import numpy as np
import ml_dtypes


def mxq(x, axis, fmt="e4m3"):
    dtype, down = {"e4m3": (ml_dtypes.float8_e4m3fn, 7), "e5m2": (ml_dtypes.float8_e5m2, 14)}[fmt]
    v = np.moveaxis(np.asarray(x, np.float32).astype(ml_dtypes.bfloat16).astype(np.float64), axis, -1)
    blocks = v.reshape(v.shape[:-1] + (-1, 32))
    amax = np.abs(blocks).max(-1, keepdims=True)
    byte = np.maximum(np.where(amax > 0, np.frexp(amax)[1] - 1 + 127, 0) - down, 1)
    scale = np.exp2(byte - 127.0)
    codes = (blocks / scale).astype(np.float32).astype(dtype).astype(np.float64)
    return np.moveaxis((codes * scale).reshape(v.shape), -1, axis)


WIDE = False


def mx_kscale(k):
    if not WIDE:
        return np.ones(k)
    levels = np.array([10, -10, 5, -5, 0])
    if k % 512:
        return np.exp2(np.random.permutation(np.resize(levels, k // 32))).repeat(32)
    a = np.empty((k // 512, 16))
    for p in range(k // 512):
        a[p, :8] = np.random.permutation(np.resize(levels, 8))
        for g in range(8):
            far = levels[np.abs(levels - a[p, g]) >= 10]
            a[p, g + 8] = far[np.random.randint(len(far))]
    return np.exp2(a.ravel()).repeat(32)


def f64(x):
    return np.asarray(x).astype(np.float64)


def striped(idx):
    return np.tile(np.asarray(idx).reshape(-1, 16).T, (8, 1)).astype(np.uint16)


def unstriped(offs):
    return offs[:16].T.reshape(-1).astype(np.int64)


E2M1 = np.array([0.0, 0.5, 1.0, 1.5, 2.0, 3.0, 4.0, 6.0, -0.0, -0.5, -1.0, -1.5, -2.0, -3.0, -4.0, -6.0])


def pack_weight(w, fmt):
    k, n = w.shape
    w = f64(np.asarray(w, np.float32).astype(ml_dtypes.bfloat16)).reshape(k // 32, 32, n)
    amax = np.abs(w).max(1)
    if fmt == "e4m3":
        byte = np.frexp(amax)[1] - 1 + 127 - 7
    else:
        mant, ex = np.frexp(amax / 6.0)
        byte = np.where(mant > 0.5, ex, ex - 1) + 127
    byte = np.clip(np.where(amax > 0, byte, 1), 1, 254)
    scaled = (w * np.exp2(127.0 - byte)[:, None, :]).reshape(k, n).astype(np.float32)
    by_word = np.ascontiguousarray(scaled.reshape(k // 512, 128, 4, n).transpose(0, 1, 3, 2))
    if fmt == "e4m3":
        words = by_word.astype(ml_dtypes.float8_e4m3fn).view(np.uint8)
    else:
        c = by_word.astype(ml_dtypes.float4_e2m1fn).view(np.uint8) & 0xF
        words = (c[..., 0::2] | (c[..., 1::2] << 4)).reshape(k // 512, 128, 2 * n)
    return np.ascontiguousarray(words), np.ascontiguousarray(byte.astype(np.uint8).reshape(k // 512, 16, n))


def unpack_weight(words, scales, fmt):
    g, _, n = scales.shape
    words = np.ascontiguousarray(words).reshape(g, 128, n, -1)
    if fmt == "e4m3":
        vals = words.view(ml_dtypes.float8_e4m3fn).astype(np.float64)
    else:
        nib = np.empty((g, 128, n, 4), np.uint8)
        nib[..., 0::2] = words & 0xF
        nib[..., 1::2] = words >> 4
        vals = E2M1[nib]
    vals = vals * np.repeat(np.exp2(scales.astype(np.float64) - 127.0), 8, axis=1)[..., None]
    return vals.transpose(0, 1, 3, 2).reshape(g * 512, n)


def bf(x):
    return np.asarray(x, np.float32).astype(ml_dtypes.bfloat16)


def planes(Y):
    r, m = Y.shape
    b = f64(bf(Y)).reshape(r // 32, 32, m)
    amax = np.abs(b).max(1)
    byte = np.clip(np.where(amax > 0, np.frexp(amax)[1] - 1 + 127 - 7, 1), 1, 254)
    codes = (b * np.exp2(127.0 - byte)[:, None, :]).reshape(r, m).astype(np.float32).astype(ml_dtypes.float8_e4m3fn).view(np.uint8)
    words = codes.reshape(r // 512, 128, 4, m).transpose(0, 1, 3, 2)
    return np.ascontiguousarray(words), np.ascontiguousarray(byte.astype(np.uint8).reshape(r // 512, 16, m))


D, T, I, Q, E = 512, 2048, 512, 256, 512


def setup_inputs():
    n = np.random.standard_normal
    idx = np.random.permutation(T)[:I]
    idx2 = np.random.randint(0, I, I)
    idx3 = np.random.randint(0, I, I)
    fd = mx_kscale(D)
    fi = mx_kscale(I)
    ti = np.ones(T)
    ti[idx] = fi
    keysp = pack_weight(n((D, T)) / fd[:, None], "e2m1")
    return {
        "query": (n((D, Q)) * 0.25 / np.sqrt(D) * fd[:, None]).astype(np.float32),
        "keys_words": keysp[0],
        "keys_scales": keysp[1],
        "sa": (np.random.uniform(0.3, 0.9, (1, I))).astype(np.float32),
        "sb": (np.random.uniform(-0.7, 0.7, (1, I))).astype(np.float32),
        "size": (np.random.uniform(0.5, 2.0, (1, I)) * fi).astype(np.float32),
        "vals": (n((E, T)) / ti).astype(np.float32),
        "offs": striped(idx),
        "offs2": striped(idx2),
        "offs3": striped(idx3),
    }


def reference(query, keys_words, keys_scales, sa, sb, size, vals, offs, offs2, offs3):
    idx = unstriped(offs)
    idx2 = unstriped(offs2)
    idx3 = unstriped(offs3)
    keysu = unpack_weight(keys_words, keys_scales, "e2m1")
    queryq = mxq(f64(query), 0, "e4m3")
    keysidxg = keysu[:, idx]
    a = queryq.T @ keysidxg
    s = a + a[:, idx2] * f64(sa) + a[:, idx3] * f64(sb)
    p = np.exp(s - np.max(s, axis=1, keepdims=True))
    w = p * f64(size) / np.sum(p, axis=1, keepdims=True)
    wt = w.T
    vt = f64(vals)[:, idx].T
    vtq = mxq(vt, 0, "e4m3")
    wtq = mxq(wt, 0, "e4m3")
    o = vtq.T @ wtq
    words, scales = planes(o)
    return o, words, scales

@@ -1,0 +1,264 @@
+from contextlib import ExitStack
+
+import concourse.mybir as mybir
+from concourse.masks import make_identity
+
+D, T, I, Q, E = 512, 2048, 512, 256, 512
+FLOPS = 2 * D * Q * I + 2 * I * E * Q
+
+F32 = mybir.dt.float32
+BF16 = mybir.dt.bfloat16
+I32 = mybir.dt.int32
+U32 = mybir.dt.uint32
+U16 = mybir.dt.uint16
+U8 = mybir.dt.uint8
+FP8X4 = mybir.dt.float8_e4m3fn_x4
+FP4X4 = mybir.dt.float4_e2m1fn_x4
+ALU = mybir.AluOpType
+ACT = mybir.ActivationFunctionType
+AX = mybir.AxisListType
+
+P = 128
+PACK = 4
+QB = Q // P
+SPARE = 32
+Q_ON_VECTOR = 160
+
+
+def tile_attend_neighbourscores_pl_kernel(
+    tc, query, keys_words, keys_scales, sa, sb, size, vals, offs, offs2, offs3, out_0, out_1, out_2
+):
+    nc = tc.nc
+    with ExitStack() as ctx:
+        lists = ctx.enter_context(tc.tile_pool(name="lists", bufs=1))
+        keep = ctx.enter_context(tc.tile_pool(name="keep", bufs=1))
+        psum = ctx.enter_context(tc.psum_pool(name="psum", bufs=1))
+        ring = ctx.enter_context(tc.psum_pool(name="ring", bufs=3))
+
+        def sb_tile(shape, dtype, name, tag=None):
+            return keep.tile(shape, dtype, name=name, tag=tag or name, align_bytes=64)
+
+        idx = lists.tile([P, I // 16], U16, name="idx")
+        idx2 = lists.tile([P, I // 16], U16, name="idx2")
+        idx3 = lists.tile([P, I // 16], U16, name="idx3")
+        ks_pool = sb_tile([P, T], U8, "ks_pool")
+        kw_pool = sb_tile([P, T], U16, "kw_pool")
+        q_raw = sb_tile([P, PACK, Q], F32, "q_raw")
+        v_pool = [sb_tile([P, T], F32, f"v_pool{t}") for t in range(PACK)]
+        warm = sb_tile([P, 1], F32, "warm")
+        warm_out = sb_tile([P, 1], F32, "warm_out")
+
+        cols = {name: sb_tile([P, PACK], F32, name + "_col") for name in ("sa", "sb", "size")}
+        vals_dealt = vals.rearrange("(m t) c -> t m c", t=PACK)
+
+        def load_col(name, vec):
+            nc.sync.dma_start(cols[name][:], vec[0].rearrange("(p r) -> p r", r=PACK))
+
+        nc.sync.dma_start(idx[:], offs)
+        load_col("sa", sa)
+        for g in range(4):
+            nc.sync.dma_start(
+                ks_pool[32 * g : 32 * g + 32, :].bitcast(I32),
+                keys_scales[0, 4 * g : 4 * g + 4, :].bitcast(I32).partition_broadcast(8),
+            )
+        nc.sync.dma_start(kw_pool[:].bitcast(I32), keys_words[0].bitcast(I32))
+        nc.sync.dma_start(q_raw[:], query.rearrange("(p j) q -> p j q", j=PACK))
+        load_col("sb", sb)
+        nc.sync.dma_start(idx2[:], offs2)
+        nc.sync.dma_start(idx3[:], offs3)
+        nc.sync.dma_start(v_pool[0][:], vals_dealt[0])
+        load_col("size", size)
+        for t in range(1, PACK):
+            nc.sync.dma_start(v_pool[t][:], vals_dealt[t])
+
+        nc.vector.memset(warm[:], 0.0)
+        nc.scalar.activation(warm_out[:], warm[:], ACT.Exp)
+        ident = sb_tile([P, P], F32, "ident")
+        make_identity(nc, ident[:])
+        a_sb = [sb_tile([P, I + SPARE], F32, f"a_sb{b}") for b in range(QB)]
+        for b in range(QB):
+            nc.gpsimd.memset(a_sb[b][:, I:], 0.0)
+
+        ks = sb_tile([P, I], U8, "ks")
+        kw = sb_tile([P, I], U16, "kw")
+        nc.vector.tensor_copy(ks[:], ks_pool[:].indirect(idx[:]))
+        nc.vector.tensor_copy(kw[:], kw_pool[:].indirect(idx[:]))
+
+        def spread(name, tag):
+            bank = psum.tile([P, PACK, P], F32, name=name + "_ps", tag=tag)
+            for r in range(PACK):
+                nc.tensor.transpose(bank[:, r, :], cols[name][:, r : r + 1].to_broadcast([P, P]), ident[:])
+            return bank[:].rearrange("q r n -> q n r")
+
+        rows = {}
+
+        def spread_to_sbuf(name, tag):
+            rows[name] = sb_tile([P, I], F32, name + "_row")
+            nc.scalar.copy(rows[name][:].rearrange("q (n r) -> q n r", r=PACK), spread(name, tag))
+
+        spread_to_sbuf("sa", "turn0")
+
+        q_grp, q_codes, q_scales = [], [], []
+        for b in range(QB):
+            q_grp.append(sb_tile([P, P * PACK], BF16, f"q_grp{b}"))
+            dst = q_grp[b][:].rearrange("p (c i j) -> p c j i", i=4, j=PACK)
+            src = q_raw[:, :, b * P : (b + 1) * P].rearrange("p j (c i) -> p c j i", i=4)
+            if b == 1:
+                nc.scalar.copy(dst, src)
+            else:
+                nc.vector.tensor_copy(dst, src)
+        for b in range(QB):
+            q_codes.append(sb_tile([P, P], U32, f"q_codes{b}"))
+            q_scales.append(sb_tile([P, P], U8, f"q_scales{b}"))
+            nc.vector.quantize_mx(out=q_codes[b][:].bitcast(FP8X4), scales=q_scales[b][:], in_=q_grp[b][:])
+
+        def scores(b, bank, cs, copy):
+            nc.tensor.matmul_mx(
+                out=bank[:],
+                lhsT=q_codes[b][:].bitcast(FP8X4),
+                lhsT_scale=q_scales[b][:],
+                rhs=kw[:, cs].bitcast(FP4X4),
+                rhs_scale=ks[:, cs],
+                start=True,
+                stop=True,
+            )
+            copy(a_sb[b][:, cs], bank[:])
+
+        scores(0, psum.tile([P, I // 2], F32, name="a_lo", tag="main0"), slice(0, I // 2), nc.scalar.copy)
+        scores(0, ring.tile([P, I // 2], F32, name="a_hi", tag="vT_ps"), slice(I // 2, I), nc.vector.tensor_copy)
+        scores(1, psum.tile([P, I], F32, name="a_ps1", tag="main1"), slice(0, I), nc.scalar.copy)
+        spread_to_sbuf("sb", "turn1")
+        size_row = spread("size", "size")
+
+        s_ps = []
+        sT_sb = []
+        sT_ps = []
+        for b in range(QB):
+            t2 = sb_tile([P, I], F32, f"t2_{b}")
+            t3 = sb_tile([P, I], F32, f"t3_{b}")
+            nc.vector.tensor_tensor(t2[:], a_sb[b][:].indirect(idx2[:]), rows["sa"][:], ALU.mult)
+            nc.vector.tensor_tensor(t3[:], a_sb[b][:].indirect(idx3[:]), rows["sb"][:], ALU.mult)
+            sT_ps.append(psum.tile([P, I], F32, name=f"sT_ps{b}", tag=f"turn{b}"))
+            terms = (a_sb[b], t2, t3)
+            for k, term in enumerate(terms):
+                for c in range(I // P):
+                    nc.tensor.matmul(
+                        sT_ps[b][:, c * P : (c + 1) * P],
+                        term[:, c * P : (c + 1) * P],
+                        ident[:],
+                        start=(k == 0 and c == 0),
+                        stop=(k == len(terms) - 1 and c == I // P - 1),
+                        is_transpose=True,
+                    )
+
+        def turn_back(b, tag):
+            sT_sb.append(sb_tile([P, I], F32, f"sT_sb{b}", tag))
+            nc.scalar.copy(sT_sb[b][:], sT_ps[b][:])
+            s_ps.append(psum.tile([P, I], F32, name=f"s_ps{b}", tag=f"main{b}"))
+            for c in range(I // P):
+                nc.tensor.transpose(s_ps[b][:, c * P : (c + 1) * P], sT_sb[b][:, c * P : (c + 1) * P], ident[:])
+
+        probs = [sb_tile([P, I], F32, f"probs{b}") for b in range(QB)]
+        row_sum = [sb_tile([P, 1], F32, f"row_sum{b}") for b in range(QB)]
+
+        def softmax(b):
+            neg_max = sb_tile([P, 1], F32, f"neg_max{b}")
+            nc.vector.tensor_reduce(neg_max[:], s_ps[b][:], AX.X, ALU.max, negate=True)
+            nc.scalar.activation(
+                probs[b][:], s_ps[b][:], ACT.Exp, bias=neg_max[:], scale=1.0, accum_out=row_sum[b][:]
+            )
+
+        grp = sb_tile([P, (QB + PACK) * I], BF16, "grp")
+
+        def turn_pairs(src, bank, k):
+            words = src[:].bitcast(F32)
+            for u in range(2):
+                nc.tensor.transpose(bank[:, u, :], words[:, u::2], ident[:])
+            nc.scalar.copy(
+                grp[:, k * I : (k + 1) * I].bitcast(F32).rearrange("p (m u) -> p m u", u=2),
+                bank[:].rearrange("p u m -> p m u"),
+            )
+
+        def weights(b, tag):
+            inv_sum = sb_tile([P, 1], F32, f"inv_sum{b}")
+            nc.vector.reciprocal(inv_sum[:], row_sum[b][:])
+            w_bf = sb_tile([P, I], BF16, f"w_bf{b}", tag)
+            nc.vector.scalar_tensor_tensor(
+                w_bf[:].rearrange("q (n r) -> q n r", r=PACK),
+                probs[b][:].rearrange("q (n r) -> q n r", r=PACK),
+                inv_sum[:],
+                size_row,
+                ALU.mult,
+                ALU.mult,
+            )
+            turn_pairs(w_bf, psum.tile([P, 2, P], F32, name=f"wT_ps{b}", tag=f"turn{b}"), b)
+
+        def turn_values(t, vg):
+            turn_pairs(vg, ring.tile([P, 2, P], F32, name="vT_ps"), QB + t)
+
+        def values(t, tag):
+            vg = sb_tile([P, I], BF16, f"vg{t}", tag)
+            nc.vector.tensor_copy(vg[:], v_pool[t][:].indirect(idx[:]))
+            turn_values(t, vg)
+
+        v_bf_pool = sb_tile([P, T], BF16, "v_bf_pool")
+        for c in range(T // I):
+            cs = slice(c * I, (c + 1) * I)
+            nc.scalar.activation(v_bf_pool[:, cs], v_pool[0][:, cs], ACT.Copy)
+        turn_back(0, "v_pool0")
+        vg0 = sb_tile([P, I], BF16, "vg0")
+        nc.scalar.activation(vg0[:], v_bf_pool[:].indirect(idx[:]), ACT.Copy)
+        turn_back(1, "v_bf_pool")
+        softmax(0)
+        values(1, "v_pool0")
+        softmax(1)
+        turn_values(0, vg0)
+        weights(0, "v_bf_pool")
+        weights(1, None)
+        values(2, None)
+        values(3, None)
+
+        codes = sb_tile([P, (QB + PACK) * P], U32, "codes", "v_pool3")
+        scales = sb_tile([P, (QB + PACK) * P], U8, "scales")
+        for k0, k1 in ((0, 4), (4, 5), (5, 6)):
+            nc.vector.quantize_mx(
+                out=codes[:, k0 * P : k1 * P].bitcast(FP8X4),
+                scales=scales[:, k0 * P : k1 * P],
+                in_=grp[:, k0 * I : k1 * I],
+            )
+
+        o_sb = sb_tile([P, PACK, Q], F32, "o_sb")
+        out_dealt = out_0.rearrange("(m t) q -> m t q", t=PACK)
+        for t in range(PACK):
+            o_ps = psum.tile([P, Q], F32, name=f"o_ps{t}", tag=("main0", "main1", "turn0", "turn1")[t])
+            vs = slice((QB + t) * P, (QB + t + 1) * P)
+            nc.tensor.matmul_mx(
+                out=o_ps[:],
+                lhsT=codes[:, vs].bitcast(FP8X4),
+                lhsT_scale=scales[:, vs],
+                rhs=codes[:, :Q].bitcast(FP8X4),
+                rhs_scale=scales[:, :Q],
+                start=True,
+                stop=True,
+            )
+            copy = nc.scalar.copy if t % 2 == 0 else nc.vector.tensor_copy
+            copy(o_sb[:, t, :], o_ps[:])
+            nc.sync.dma_start(out_dealt[:, t, :], o_sb[:, t, :])
+
+        o_bf = sb_tile([P, Q, PACK], BF16, "o_bf")
+        for eng, qs in ((nc.vector.tensor_copy, slice(0, Q_ON_VECTOR)), (nc.scalar.copy, slice(Q_ON_VECTOR, Q))):
+            eng(
+                o_bf[:, qs, :].rearrange("p (c i) t -> p c t i", i=4),
+                o_sb[:, :, qs].rearrange("p t (c i) -> p c t i", i=4),
+            )
+        o_codes = sb_tile([P, Q], U32, "o_codes")
+        o_scales = sb_tile([P, Q], U8, "o_scales")
+        nc.vector.quantize_mx(
+            out=o_codes[:].bitcast(FP8X4), scales=o_scales[:], in_=o_bf[:].rearrange("p q t -> p (q t)")
+        )
+        nc.sync.dma_start(out_1[0].rearrange("p c r -> p (c r)").bitcast(I32), o_codes[:].bitcast(I32))
+        for g in range(4):
+            queue = nc.scalar if g % 2 == 0 else nc.sync
+            queue.dma_start(
+                out_2[0, 4 * g : 4 * g + 4, :].bitcast(I32), o_scales[32 * g : 32 * g + 4, :].bitcast(I32)
+            )

@@ -20,9 +20,12 @@ AX = mybir.AxisListType
 
 P = 128
 PACK = 4
-QB = Q // P
+QUADRANTS = 4
+BLOCKS = Q // P
+LIST_COLS = I // 16
+RUN = 4
 SPARE = 32
-Q_ON_VECTOR = 160
+ROUNDED_ON_VECTOR = 88
 
 
 def tile_attend_neighbourscores_pl_kernel(
@@ -35,34 +38,33 @@ def tile_attend_neighbourscores_pl_kernel(
         psum = ctx.enter_context(tc.psum_pool(name="psum", bufs=1))
         ring = ctx.enter_context(tc.psum_pool(name="ring", bufs=3))
 
-        def sb_tile(shape, dtype, name, tag=None):
-            return keep.tile(shape, dtype, name=name, tag=tag or name, align_bytes=64)
+        def sbuf(shape, dtype, name, slot_of=None):
+            return keep.tile(shape, dtype, name=name, tag=slot_of or name, align_bytes=64)
 
-        idx = lists.tile([P, I // 16], U16, name="idx")
-        idx2 = lists.tile([P, I // 16], U16, name="idx2")
-        idx3 = lists.tile([P, I // 16], U16, name="idx3")
-        ks_pool = sb_tile([P, T], U8, "ks_pool")
-        kw_pool = sb_tile([P, T], U16, "kw_pool")
-        q_raw = sb_tile([P, PACK, Q], F32, "q_raw")
-        v_pool = [sb_tile([P, T], F32, f"v_pool{t}") for t in range(PACK)]
-        warm = sb_tile([P, 1], F32, "warm")
-        warm_out = sb_tile([P, 1], F32, "warm_out")
-
-        cols = {name: sb_tile([P, PACK], F32, name + "_col") for name in ("sa", "sb", "size")}
+        idx = lists.tile([P, LIST_COLS], U16, name="idx")
+        idx2 = lists.tile([P, LIST_COLS], U16, name="idx2")
+        idx3 = lists.tile([P, LIST_COLS], U16, name="idx3")
+        ks_pool = sbuf([P, T], U8, "ks_pool")
+        kw_pool = sbuf([P, T], U16, "kw_pool")
+        q_raw = [sbuf([P, PACK, P], F32, f"q_raw{b}") for b in range(BLOCKS)]
+        v_pool = [sbuf([P, T], F32, f"v_pool{t}") for t in range(PACK)]
+        cols = {name: sbuf([P, PACK], F32, name + "_col") for name in ("sa", "sb", "size")}
         vals_dealt = vals.rearrange("(m t) c -> t m c", t=PACK)
+        query_rows = query.rearrange("(p r) q -> p r q", r=PACK)
 
         def load_col(name, vec):
-            nc.sync.dma_start(cols[name][:], vec[0].rearrange("(p r) -> p r", r=PACK))
+            nc.sync.dma_start(cols[name][:], vec[0].rearrange("(n r) -> n r", r=PACK))
 
         nc.sync.dma_start(idx[:], offs)
         load_col("sa", sa)
-        for g in range(4):
+        for g in range(QUADRANTS):
             nc.sync.dma_start(
                 ks_pool[32 * g : 32 * g + 32, :].bitcast(I32),
                 keys_scales[0, 4 * g : 4 * g + 4, :].bitcast(I32).partition_broadcast(8),
             )
+        nc.sync.dma_start(q_raw[0][:], query_rows[:, :, :P])
         nc.sync.dma_start(kw_pool[:].bitcast(I32), keys_words[0].bitcast(I32))
-        nc.sync.dma_start(q_raw[:], query.rearrange("(p j) q -> p j q", j=PACK))
+        nc.sync.dma_start(q_raw[1][:], query_rows[:, :, P:])
         load_col("sb", sb)
         nc.sync.dma_start(idx2[:], offs2)
         nc.sync.dma_start(idx3[:], offs3)
@@ -71,193 +73,230 @@ def tile_attend_neighbourscores_pl_kernel(
         for t in range(1, PACK):
             nc.sync.dma_start(v_pool[t][:], vals_dealt[t])
 
-        nc.vector.memset(warm[:], 0.0)
-        nc.scalar.activation(warm_out[:], warm[:], ACT.Exp)
-        ident = sb_tile([P, P], F32, "ident")
+        ident = sbuf([P, P], F32, "ident")
         make_identity(nc, ident[:])
-        a_sb = [sb_tile([P, I + SPARE], F32, f"a_sb{b}") for b in range(QB)]
-        for b in range(QB):
+        a_sb = [sbuf([P, I + SPARE], F32, f"a_sb{b}") for b in range(BLOCKS)]
+        for b in range(BLOCKS):
             nc.gpsimd.memset(a_sb[b][:, I:], 0.0)
 
-        ks = sb_tile([P, I], U8, "ks")
-        kw = sb_tile([P, I], U16, "kw")
-        nc.vector.tensor_copy(ks[:], ks_pool[:].indirect(idx[:]))
-        nc.vector.tensor_copy(kw[:], kw_pool[:].indirect(idx[:]))
-
-        def spread(name, tag):
-            bank = psum.tile([P, PACK, P], F32, name=name + "_ps", tag=tag)
-            for r in range(PACK):
-                nc.tensor.transpose(bank[:, r, :], cols[name][:, r : r + 1].to_broadcast([P, P]), ident[:])
-            return bank[:].rearrange("q r n -> q n r")
+        def spread(dst, name, r):
+            nc.tensor.transpose(dst, cols[name][:, r : r + 1].to_broadcast([P, P]), ident[:])
 
         rows = {}
 
-        def spread_to_sbuf(name, tag):
-            rows[name] = sb_tile([P, I], F32, name + "_row")
-            nc.scalar.copy(rows[name][:].rearrange("q (n r) -> q n r", r=PACK), spread(name, tag))
+        def spread_to_sbuf(name, bank_tag):
+            rows[name] = sbuf([P, I], F32, name + "_row")
+            bank = psum.tile([P, PACK, P], F32, name=name + "_ps", tag=bank_tag)
+            for r in range(PACK):
+                spread(bank[:, r, :], name, r)
+            nc.scalar.activation(
+                rows[name][:].rearrange("q (n r) -> q n r", r=PACK), bank[:].rearrange("q r n -> q n r"), ACT.Copy
+            )
 
         spread_to_sbuf("sa", "turn0")
 
-        q_grp, q_codes, q_scales = [], [], []
-        for b in range(QB):
-            q_grp.append(sb_tile([P, P * PACK], BF16, f"q_grp{b}"))
-            dst = q_grp[b][:].rearrange("p (c i j) -> p c j i", i=4, j=PACK)
-            src = q_raw[:, :, b * P : (b + 1) * P].rearrange("p j (c i) -> p c j i", i=4)
-            if b == 1:
-                nc.scalar.copy(dst, src)
-            else:
-                nc.vector.tensor_copy(dst, src)
-        for b in range(QB):
-            q_codes.append(sb_tile([P, P], U32, f"q_codes{b}"))
-            q_scales.append(sb_tile([P, P], U8, f"q_scales{b}"))
-            nc.vector.quantize_mx(out=q_codes[b][:].bitcast(FP8X4), scales=q_scales[b][:], in_=q_grp[b][:])
+        ks = sbuf([P, I], U8, "ks")
+        kw = sbuf([P, I], U16, "kw", "sa_col")
+        nc.vector.tensor_copy(ks[:], ks_pool[:].indirect(idx[:]))
 
-        def scores(b, bank, cs, copy):
+        def quantise(src, name, slot_of=None):
+            width = src.shape[1] // PACK
+            codes = sbuf([P, width], U32, name + "_codes", slot_of)
+            scales = sbuf([P, width], U8, name + "_scales")
+            nc.vector.quantize_mx(out=codes[:].bitcast(FP8X4), scales=scales[:], in_=src)
+            return codes, scales
+
+        def quantise_queries(b, slot_of=None):
+            q_grp = sbuf([P, P * PACK], BF16, f"q_grp{b}")
+            nc.scalar.activation(
+                q_grp[:].rearrange("p (c j r) -> p c r j", j=RUN, r=PACK),
+                q_raw[b][:].rearrange("p r (c j) -> p c r j", j=RUN),
+                ACT.Copy,
+            )
+            return quantise(q_grp[:], f"q{b}", slot_of)
+
+        halves = (slice(0, I // 2), slice(I // 2, I))
+        q_mx = [quantise_queries(0)]
+        for h, slots in enumerate(halves):
+            half_list = idx[:, h * LIST_COLS // 2 : (h + 1) * LIST_COLS // 2]
+            nc.vector.tensor_copy(kw[:, slots], kw_pool[:].indirect(half_list))
+        q_mx.append(quantise_queries(1, "kw_pool"))
+
+        def scores(b, bank, slots):
             nc.tensor.matmul_mx(
                 out=bank[:],
-                lhsT=q_codes[b][:].bitcast(FP8X4),
-                lhsT_scale=q_scales[b][:],
-                rhs=kw[:, cs].bitcast(FP4X4),
-                rhs_scale=ks[:, cs],
+                lhsT=q_mx[b][0][:].bitcast(FP8X4),
+                lhsT_scale=q_mx[b][1][:],
+                rhs=kw[:, slots].bitcast(FP4X4),
+                rhs_scale=ks[:, slots],
                 start=True,
                 stop=True,
             )
-            copy(a_sb[b][:, cs], bank[:])
+            nc.scalar.copy(a_sb[b][:, slots], bank[:])
 
-        scores(0, psum.tile([P, I // 2], F32, name="a_lo", tag="main0"), slice(0, I // 2), nc.scalar.copy)
-        scores(0, ring.tile([P, I // 2], F32, name="a_hi", tag="vT_ps"), slice(I // 2, I), nc.vector.tensor_copy)
-        scores(1, psum.tile([P, I], F32, name="a_ps1", tag="main1"), slice(0, I), nc.scalar.copy)
+        scores(0, psum.tile([P, I // 2], F32, name="a_lo", tag="main0"), halves[0])
+        scores(0, ring.tile([P, I // 2], F32, name="a_hi", tag="ring"), halves[1])
+        scores(1, psum.tile([P, I], F32, name="a_ps1", tag="main1"), slice(0, I))
         spread_to_sbuf("sb", "turn1")
-        size_row = spread("size", "size")
+        size_row = psum.tile([P, 2, P, 2], F32, name="size_row")
+        for r in range(PACK):
+            spread(size_row[:, r // 2, :, r % 2], "size", r)
 
-        s_ps = []
-        sT_sb = []
+        linked = {}
+        for name, links, row in (("t2", idx2, "sa"), ("t3", idx3, "sb")):
+            for b in range(BLOCKS):
+                linked[name, b] = sbuf([P, I], F32, f"{name}_{b}")
+                nc.vector.tensor_tensor(linked[name, b][:], a_sb[b][:].indirect(links[:]), rows[row][:], ALU.mult)
+        chunks = [slice(c * P, (c + 1) * P) for c in range(I // P)]
         sT_ps = []
-        for b in range(QB):
-            t2 = sb_tile([P, I], F32, f"t2_{b}")
-            t3 = sb_tile([P, I], F32, f"t3_{b}")
-            nc.vector.tensor_tensor(t2[:], a_sb[b][:].indirect(idx2[:]), rows["sa"][:], ALU.mult)
-            nc.vector.tensor_tensor(t3[:], a_sb[b][:].indirect(idx3[:]), rows["sb"][:], ALU.mult)
+        for b in range(BLOCKS):
             sT_ps.append(psum.tile([P, I], F32, name=f"sT_ps{b}", tag=f"turn{b}"))
-            terms = (a_sb[b], t2, t3)
-            for k, term in enumerate(terms):
-                for c in range(I // P):
-                    nc.tensor.matmul(
-                        sT_ps[b][:, c * P : (c + 1) * P],
-                        term[:, c * P : (c + 1) * P],
-                        ident[:],
-                        start=(k == 0 and c == 0),
-                        stop=(k == len(terms) - 1 and c == I // P - 1),
-                        is_transpose=True,
-                    )
+            passes = [(term, c) for term in (a_sb[b], linked["t2", b], linked["t3", b]) for c in chunks]
+            for n, (term, c) in enumerate(passes):
+                nc.tensor.matmul(
+                    sT_ps[b][:, c],
+                    term[:, c],
+                    ident[:],
+                    start=(n == 0),
+                    stop=(n == len(passes) - 1),
+                    is_transpose=True,
+                )
 
-        def turn_back(b, tag):
-            sT_sb.append(sb_tile([P, I], F32, f"sT_sb{b}", tag))
-            nc.scalar.copy(sT_sb[b][:], sT_ps[b][:])
-            s_ps.append(psum.tile([P, I], F32, name=f"s_ps{b}", tag=f"main{b}"))
-            for c in range(I // P):
-                nc.tensor.transpose(s_ps[b][:, c * P : (c + 1) * P], sT_sb[b][:, c * P : (c + 1) * P], ident[:])
-
-        probs = [sb_tile([P, I], F32, f"probs{b}") for b in range(QB)]
-        row_sum = [sb_tile([P, 1], F32, f"row_sum{b}") for b in range(QB)]
-
-        def softmax(b):
-            neg_max = sb_tile([P, 1], F32, f"neg_max{b}")
-            nc.vector.tensor_reduce(neg_max[:], s_ps[b][:], AX.X, ALU.max, negate=True)
-            nc.scalar.activation(
-                probs[b][:], s_ps[b][:], ACT.Exp, bias=neg_max[:], scale=1.0, accum_out=row_sum[b][:]
-            )
-
-        grp = sb_tile([P, (QB + PACK) * I], BF16, "grp")
-
-        def turn_pairs(src, bank, k):
-            words = src[:].bitcast(F32)
-            for u in range(2):
-                nc.tensor.transpose(bank[:, u, :], words[:, u::2], ident[:])
-            nc.scalar.copy(
-                grp[:, k * I : (k + 1) * I].bitcast(F32).rearrange("p (m u) -> p m u", u=2),
-                bank[:].rearrange("p u m -> p m u"),
-            )
-
-        def weights(b, tag):
-            inv_sum = sb_tile([P, 1], F32, f"inv_sum{b}")
-            nc.vector.reciprocal(inv_sum[:], row_sum[b][:])
-            w_bf = sb_tile([P, I], BF16, f"w_bf{b}", tag)
-            nc.vector.scalar_tensor_tensor(
-                w_bf[:].rearrange("q (n r) -> q n r", r=PACK),
-                probs[b][:].rearrange("q (n r) -> q n r", r=PACK),
-                inv_sum[:],
-                size_row,
-                ALU.mult,
-                ALU.mult,
-            )
-            turn_pairs(w_bf, psum.tile([P, 2, P], F32, name=f"wT_ps{b}", tag=f"turn{b}"), b)
-
-        def turn_values(t, vg):
-            turn_pairs(vg, ring.tile([P, 2, P], F32, name="vT_ps"), QB + t)
-
-        def values(t, tag):
-            vg = sb_tile([P, I], BF16, f"vg{t}", tag)
-            nc.vector.tensor_copy(vg[:], v_pool[t][:].indirect(idx[:]))
-            turn_values(t, vg)
-
-        v_bf_pool = sb_tile([P, T], BF16, "v_bf_pool")
+        v_bf_pool = sbuf([P, T], BF16, "v_bf_pool", "sa_col")
         for c in range(T // I):
-            cs = slice(c * I, (c + 1) * I)
-            nc.scalar.activation(v_bf_pool[:, cs], v_pool[0][:, cs], ACT.Copy)
-        turn_back(0, "v_pool0")
-        vg0 = sb_tile([P, I], BF16, "vg0")
-        nc.scalar.activation(vg0[:], v_bf_pool[:].indirect(idx[:]), ACT.Copy)
-        turn_back(1, "v_bf_pool")
-        softmax(0)
-        values(1, "v_pool0")
-        softmax(1)
-        turn_values(0, vg0)
-        weights(0, "v_bf_pool")
-        weights(1, None)
-        values(2, None)
-        values(3, None)
+            piece = slice(c * I, (c + 1) * I)
+            nc.scalar.activation(v_bf_pool[:, piece], v_pool[0][:, piece], ACT.Copy)
 
-        codes = sb_tile([P, (QB + PACK) * P], U32, "codes", "v_pool3")
-        scales = sb_tile([P, (QB + PACK) * P], U8, "scales")
-        for k0, k1 in ((0, 4), (4, 5), (5, 6)):
-            nc.vector.quantize_mx(
-                out=codes[:, k0 * P : k1 * P].bitcast(FP8X4),
-                scales=scales[:, k0 * P : k1 * P],
-                in_=grp[:, k0 * I : k1 * I],
-            )
+        sT_sb = sbuf([P, BLOCKS * I], F32, "sT_sb", "v_pool0")
+        s_ps = []
+        for b in range(BLOCKS):
+            turned = sT_sb[:, b * I : (b + 1) * I]
+            nc.scalar.copy(turned, sT_ps[b][:])
+            s_ps.append(psum.tile([P, I], F32, name=f"s_ps{b}", tag=f"main{b}"))
+            for c in chunks:
+                nc.tensor.transpose(s_ps[b][:, c], turned[:, c], ident[:])
 
-        o_sb = sb_tile([P, PACK, Q], F32, "o_sb")
-        out_dealt = out_0.rearrange("(m t) q -> m t q", t=PACK)
-        for t in range(PACK):
-            o_ps = psum.tile([P, Q], F32, name=f"o_ps{t}", tag=("main0", "main1", "turn0", "turn1")[t])
-            vs = slice((QB + t) * P, (QB + t + 1) * P)
-            nc.tensor.matmul_mx(
-                out=o_ps[:],
-                lhsT=codes[:, vs].bitcast(FP8X4),
-                lhsT_scale=scales[:, vs],
-                rhs=codes[:, :Q].bitcast(FP8X4),
-                rhs_scale=scales[:, :Q],
-                start=True,
-                stop=True,
-            )
-            copy = nc.scalar.copy if t % 2 == 0 else nc.vector.tensor_copy
-            copy(o_sb[:, t, :], o_ps[:])
-            nc.sync.dma_start(out_dealt[:, t, :], o_sb[:, t, :])
+        def turn_pairs(src, bank, sorted_pairs):
+            pairs = src[:].bitcast(F32)
+            for u in range(2):
+                part = pairs[:, u * P : (u + 1) * P] if sorted_pairs else pairs[:, u::2]
+                nc.tensor.transpose(bank[:, u, :], part, ident[:])
 
-        o_bf = sb_tile([P, Q, PACK], BF16, "o_bf")
-        for eng, qs in ((nc.vector.tensor_copy, slice(0, Q_ON_VECTOR)), (nc.scalar.copy, slice(Q_ON_VECTOR, Q))):
-            eng(
-                o_bf[:, qs, :].rearrange("p (c i) t -> p c t i", i=4),
-                o_sb[:, :, qs].rearrange("p t (c i) -> p c t i", i=4),
-            )
-        o_codes = sb_tile([P, Q], U32, "o_codes")
-        o_scales = sb_tile([P, Q], U8, "o_scales")
-        nc.vector.quantize_mx(
-            out=o_codes[:].bitcast(FP8X4), scales=o_scales[:], in_=o_bf[:].rearrange("p q t -> p (q t)")
+        def interleave(dst, bank):
+            nc.scalar.copy(dst.bitcast(F32).rearrange("p (m u) -> p m u", u=2), bank.rearrange("p u m -> p m u"))
+
+        def gather_values(t, slot_of):
+            vg = sbuf([P, I], BF16, f"vg{t}", slot_of)
+            nc.vector.tensor_copy(vg[:], v_pool[t][:].indirect(idx[:]))
+            return vg
+
+        vg0 = sbuf([P, I], BF16, "vg0", "t3_1")
+        nc.scalar.activation(
+            vg0[:].rearrange("m (u p v) -> m p u v", u=2, v=2), v_bf_pool[:].indirect(idx[:]), ACT.Copy
         )
+        vg = [vg0, gather_values(1, "t2_0"), gather_values(2, "t3_0")]
+
+        neg_max = sbuf([P, BLOCKS], F32, "neg_max", "v_pool2")
+        probs = [sbuf([P, I], F32, f"probs{b}") for b in range(BLOCKS)]
+        row_sum = sbuf([P, BLOCKS], F32, "row_sum")
+        for b in range(BLOCKS):
+            nc.vector.tensor_reduce(neg_max[:, b : b + 1], s_ps[b][:], AX.X, ALU.max, negate=True)
+            nc.scalar.activation(
+                probs[b][:].rearrange("q (u n v) -> q u n v", u=2, v=2),
+                s_ps[b][:].rearrange("q (n u v) -> q u n v", u=2, v=2),
+                ACT.Exp,
+                bias=neg_max[:, b : b + 1],
+                scale=1.0,
+                accum_out=row_sum[:, b : b + 1],
+            )
+
+        vT12 = psum.tile([P, 2, 2, P], F32, name="vT12", tag="turn1")
+        vT = [ring.tile([P, 2, P], F32, name="vT0", tag="ring")[:], vT12[:, 0], vT12[:, 1]]
+        v_grp = sbuf([P, PACK * I], BF16, "v_grp", "v_pool2")
+        for t in (1, 2, 0):
+            turn_pairs(vg[t], vT[t], sorted_pairs=(t == 0))
+        for t in range(PACK - 1):
+            interleave(v_grp[:, t * I : (t + 1) * I], vT[t])
+
+        vg3 = gather_values(3, "t3_0")
+        inv_sum = sbuf([P, BLOCKS], F32, "inv_sum", "v_pool3")
+        nc.vector.reciprocal(inv_sum[:], row_sum[:])
+        v_mx = [quantise(v_grp[:, : 2 * I], "v01", "row_sum")]
+        vT3 = ring.tile([P, 2, P], F32, name="vT3", tag="ring")
+        turn_pairs(vg3, vT3[:], sorted_pairs=False)
+        interleave(v_grp[:, 3 * I :], vT3[:])
+
+        w_grp = []
+        for b in range(BLOCKS):
+            w_bf = sbuf([P, I], BF16, f"w_bf{b}")
+            nc.vector.scalar_tensor_tensor(
+                w_bf[:],
+                probs[b][:],
+                inv_sum[:, b : b + 1],
+                size_row[:].rearrange("q u n v -> q (u n v)"),
+                ALU.mult,
+                ALU.mult,
+            )
+            wT_ps = psum.tile([P, 2, P], F32, name=f"wT_ps{b}", tag=f"turn{b}")
+            w_grp.append(sbuf([P, I], BF16, f"w_grp{b}"))
+            turn_pairs(w_bf, wT_ps[:], sorted_pairs=True)
+            interleave(w_grp[b][:], wT_ps[:])
+        v_mx.append(quantise(v_grp[:, 2 * I :], "v23", "probs0"))
+        w_mx = [quantise(w_grp[b][:], f"w{b}") for b in range(BLOCKS)]
+
+        def products(b, bank, tiles):
+            for n, t in enumerate(tiles):
+                features = slice((t % 2) * P, (t % 2 + 1) * P)
+                nc.tensor.matmul_mx(
+                    out=bank[:, n, :],
+                    lhsT=v_mx[t // 2][0][:, features].bitcast(FP8X4),
+                    lhsT_scale=v_mx[t // 2][1][:, features],
+                    rhs=w_mx[b][0][:].bitcast(FP8X4),
+                    rhs_scale=w_mx[b][1][:],
+                    start=True,
+                    stop=True,
+                )
+
+        out_dealt = out_0.rearrange("(m t) q -> m t q", t=PACK)
+        o_sb = [sbuf([P, PACK, P], F32, f"o_sb{b}") for b in range(BLOCKS)]
+        o_codes = sbuf([P, Q], U32, "o_codes")
+        o_scales = sbuf([P, Q], U8, "o_scales")
+
+        def quantise_result(b, rounded):
+            block = slice(b * P, (b + 1) * P)
+            nc.vector.quantize_mx(
+                out=o_codes[:, block].bitcast(FP8X4),
+                scales=o_scales[:, block],
+                in_=rounded[:].rearrange("p q t -> p (q t)"),
+            )
+
+        o_ps0 = psum.tile([P, PACK, P], F32, name="o_ps0", tag="main0")
+        products(0, o_ps0, range(PACK))
+        o_bf0 = sbuf([P, P, PACK], BF16, "o_bf0", "w_grp1")
+        nc.vector.tensor_copy(o_bf0[:], o_ps0[:].rearrange("p t q -> p q t"))
+        o_lo = psum.tile([P, 2, P], F32, name="o_lo", tag="main1")
+        o_hi = ring.tile([P, 2, P], F32, name="o_hi", tag="ring")
+        products(1, o_lo, (0, 1))
+        products(1, o_hi, (2, 3))
+        nc.scalar.copy(o_sb[1][:, :2, :], o_lo[:])
+        nc.vector.tensor_copy(o_sb[1][:, 2:, :], o_hi[:])
+        nc.sync.dma_start(out_dealt[:, :, P:], o_sb[1][:])
+        nc.scalar.copy(o_sb[0][:], o_ps0[:])
+        nc.sync.dma_start(out_dealt[:, :, :P], o_sb[0][:])
+        quantise_result(0, o_bf0)
+        o_bf1 = sbuf([P, P, PACK], BF16, "o_bf1")
+        for copy, share in (
+            (nc.vector.tensor_copy, slice(0, ROUNDED_ON_VECTOR)),
+            (nc.scalar.copy, slice(ROUNDED_ON_VECTOR, P)),
+        ):
+            copy(
+                o_bf1[:, share, :].rearrange("p (c j) t -> p c t j", j=RUN),
+                o_sb[1][:, :, share].rearrange("p t (c j) -> p c t j", j=RUN),
+            )
+        quantise_result(1, o_bf1)
+
         nc.sync.dma_start(out_1[0].rearrange("p c r -> p (c r)").bitcast(I32), o_codes[:].bitcast(I32))
-        for g in range(4):
+        for g in range(QUADRANTS):
             queue = nc.scalar if g % 2 == 0 else nc.sync
             queue.dma_start(
                 out_2[0, 4 * g : 4 * g + 4, :].bitcast(I32), o_scales[32 * g : 32 * g + 4, :].bitcast(I32)

from contextlib import ExitStack

import concourse.mybir as mybir
from concourse.masks import make_identity

D, T, I, Q, E = 512, 2048, 512, 256, 512
FLOPS = 2 * D * Q * I + 2 * I * E * Q

F32 = mybir.dt.float32
BF16 = mybir.dt.bfloat16
I32 = mybir.dt.int32
U32 = mybir.dt.uint32
U16 = mybir.dt.uint16
U8 = mybir.dt.uint8
FP8X4 = mybir.dt.float8_e4m3fn_x4
FP4X4 = mybir.dt.float4_e2m1fn_x4
ALU = mybir.AluOpType
ACT = mybir.ActivationFunctionType
AX = mybir.AxisListType

P = 128
PACK = 4
QUADRANTS = 4
BLOCKS = Q // P
LIST_COLS = I // 16
RUN = 4
SPARE = 32
ROUNDED_ON_VECTOR = 88


def tile_attend_neighbourscores_pl_kernel(
    tc, query, keys_words, keys_scales, sa, sb, size, vals, offs, offs2, offs3, out_0, out_1, out_2
):
    nc = tc.nc
    with ExitStack() as ctx:
        lists = ctx.enter_context(tc.tile_pool(name="lists", bufs=1))
        keep = ctx.enter_context(tc.tile_pool(name="keep", bufs=1))
        psum = ctx.enter_context(tc.psum_pool(name="psum", bufs=1))
        ring = ctx.enter_context(tc.psum_pool(name="ring", bufs=3))

        def sbuf(shape, dtype, name, slot_of=None):
            return keep.tile(shape, dtype, name=name, tag=slot_of or name, align_bytes=64)

        idx = lists.tile([P, LIST_COLS], U16, name="idx")
        idx2 = lists.tile([P, LIST_COLS], U16, name="idx2")
        idx3 = lists.tile([P, LIST_COLS], U16, name="idx3")
        ks_pool = sbuf([P, T], U8, "ks_pool")
        kw_pool = sbuf([P, T], U16, "kw_pool")
        q_raw = [sbuf([P, PACK, P], F32, f"q_raw{b}") for b in range(BLOCKS)]
        v_pool = [sbuf([P, T], F32, f"v_pool{t}") for t in range(PACK)]
        cols = {name: sbuf([P, PACK], F32, name + "_col") for name in ("sa", "sb", "size")}
        vals_dealt = vals.rearrange("(m t) c -> t m c", t=PACK)
        query_rows = query.rearrange("(p r) q -> p r q", r=PACK)

        def load_col(name, vec):
            nc.sync.dma_start(cols[name][:], vec[0].rearrange("(n r) -> n r", r=PACK))

        nc.sync.dma_start(idx[:], offs)
        load_col("sa", sa)
        for g in range(QUADRANTS):
            nc.sync.dma_start(
                ks_pool[32 * g : 32 * g + 32, :].bitcast(I32),
                keys_scales[0, 4 * g : 4 * g + 4, :].bitcast(I32).partition_broadcast(8),
            )
        nc.sync.dma_start(q_raw[0][:], query_rows[:, :, :P])
        nc.sync.dma_start(kw_pool[:].bitcast(I32), keys_words[0].bitcast(I32))
        nc.sync.dma_start(q_raw[1][:], query_rows[:, :, P:])
        load_col("sb", sb)
        nc.sync.dma_start(idx2[:], offs2)
        nc.sync.dma_start(idx3[:], offs3)
        nc.sync.dma_start(v_pool[0][:], vals_dealt[0])
        load_col("size", size)
        for t in range(1, PACK):
            nc.sync.dma_start(v_pool[t][:], vals_dealt[t])

        ident = sbuf([P, P], F32, "ident")
        make_identity(nc, ident[:])
        a_sb = [sbuf([P, I + SPARE], F32, f"a_sb{b}") for b in range(BLOCKS)]
        for b in range(BLOCKS):
            nc.gpsimd.memset(a_sb[b][:, I:], 0.0)

        def spread(dst, name, r):
            nc.tensor.transpose(dst, cols[name][:, r : r + 1].to_broadcast([P, P]), ident[:])

        rows = {}

        def spread_to_sbuf(name, bank_tag):
            rows[name] = sbuf([P, I], F32, name + "_row")
            bank = psum.tile([P, PACK, P], F32, name=name + "_ps", tag=bank_tag)
            for r in range(PACK):
                spread(bank[:, r, :], name, r)
            nc.scalar.activation(
                rows[name][:].rearrange("q (n r) -> q n r", r=PACK), bank[:].rearrange("q r n -> q n r"), ACT.Copy
            )

        spread_to_sbuf("sa", "turn0")

        ks = sbuf([P, I], U8, "ks")
        kw = sbuf([P, I], U16, "kw", "sa_col")
        nc.vector.tensor_copy(ks[:], ks_pool[:].indirect(idx[:]))

        def quantise(src, name, slot_of=None):
            width = src.shape[1] // PACK
            codes = sbuf([P, width], U32, name + "_codes", slot_of)
            scales = sbuf([P, width], U8, name + "_scales")
            nc.vector.quantize_mx(out=codes[:].bitcast(FP8X4), scales=scales[:], in_=src)
            return codes, scales

        def quantise_queries(b, slot_of=None):
            q_grp = sbuf([P, P * PACK], BF16, f"q_grp{b}")
            nc.scalar.activation(
                q_grp[:].rearrange("p (c j r) -> p c r j", j=RUN, r=PACK),
                q_raw[b][:].rearrange("p r (c j) -> p c r j", j=RUN),
                ACT.Copy,
            )
            return quantise(q_grp[:], f"q{b}", slot_of)

        halves = (slice(0, I // 2), slice(I // 2, I))
        q_mx = [quantise_queries(0)]
        for h, slots in enumerate(halves):
            half_list = idx[:, h * LIST_COLS // 2 : (h + 1) * LIST_COLS // 2]
            nc.vector.tensor_copy(kw[:, slots], kw_pool[:].indirect(half_list))
        q_mx.append(quantise_queries(1, "kw_pool"))

        def scores(b, bank, slots):
            nc.tensor.matmul_mx(
                out=bank[:],
                lhsT=q_mx[b][0][:].bitcast(FP8X4),
                lhsT_scale=q_mx[b][1][:],
                rhs=kw[:, slots].bitcast(FP4X4),
                rhs_scale=ks[:, slots],
                start=True,
                stop=True,
            )
            nc.scalar.copy(a_sb[b][:, slots], bank[:])

        scores(0, psum.tile([P, I // 2], F32, name="a_lo", tag="main0"), halves[0])
        scores(0, ring.tile([P, I // 2], F32, name="a_hi", tag="ring"), halves[1])
        scores(1, psum.tile([P, I], F32, name="a_ps1", tag="main1"), slice(0, I))
        spread_to_sbuf("sb", "turn1")
        size_row = psum.tile([P, 2, P, 2], F32, name="size_row")
        for r in range(PACK):
            spread(size_row[:, r // 2, :, r % 2], "size", r)

        linked = {}
        for name, links, row in (("t2", idx2, "sa"), ("t3", idx3, "sb")):
            for b in range(BLOCKS):
                linked[name, b] = sbuf([P, I], F32, f"{name}_{b}")
                nc.vector.tensor_tensor(linked[name, b][:], a_sb[b][:].indirect(links[:]), rows[row][:], ALU.mult)
        chunks = [slice(c * P, (c + 1) * P) for c in range(I // P)]
        sT_ps = []
        for b in range(BLOCKS):
            sT_ps.append(psum.tile([P, I], F32, name=f"sT_ps{b}", tag=f"turn{b}"))
            passes = [(term, c) for term in (a_sb[b], linked["t2", b], linked["t3", b]) for c in chunks]
            for n, (term, c) in enumerate(passes):
                nc.tensor.matmul(
                    sT_ps[b][:, c],
                    term[:, c],
                    ident[:],
                    start=(n == 0),
                    stop=(n == len(passes) - 1),
                    is_transpose=True,
                )

        v_bf_pool = sbuf([P, T], BF16, "v_bf_pool", "sa_col")
        for c in range(T // I):
            piece = slice(c * I, (c + 1) * I)
            nc.scalar.activation(v_bf_pool[:, piece], v_pool[0][:, piece], ACT.Copy)

        sT_sb = sbuf([P, BLOCKS * I], F32, "sT_sb", "v_pool0")
        s_ps = []
        for b in range(BLOCKS):
            turned = sT_sb[:, b * I : (b + 1) * I]
            nc.scalar.copy(turned, sT_ps[b][:])
            s_ps.append(psum.tile([P, I], F32, name=f"s_ps{b}", tag=f"main{b}"))
            for c in chunks:
                nc.tensor.transpose(s_ps[b][:, c], turned[:, c], ident[:])

        def turn_pairs(src, bank, sorted_pairs):
            pairs = src[:].bitcast(F32)
            for u in range(2):
                part = pairs[:, u * P : (u + 1) * P] if sorted_pairs else pairs[:, u::2]
                nc.tensor.transpose(bank[:, u, :], part, ident[:])

        def interleave(dst, bank):
            nc.scalar.copy(dst.bitcast(F32).rearrange("p (m u) -> p m u", u=2), bank.rearrange("p u m -> p m u"))

        def gather_values(t, slot_of):
            vg = sbuf([P, I], BF16, f"vg{t}", slot_of)
            nc.vector.tensor_copy(vg[:], v_pool[t][:].indirect(idx[:]))
            return vg

        vg0 = sbuf([P, I], BF16, "vg0", "t3_1")
        nc.scalar.activation(
            vg0[:].rearrange("m (u p v) -> m p u v", u=2, v=2), v_bf_pool[:].indirect(idx[:]), ACT.Copy
        )
        vg = [vg0, gather_values(1, "t2_0"), gather_values(2, "t3_0")]

        neg_max = sbuf([P, BLOCKS], F32, "neg_max", "v_pool2")
        probs = [sbuf([P, I], F32, f"probs{b}") for b in range(BLOCKS)]
        row_sum = sbuf([P, BLOCKS], F32, "row_sum")
        for b in range(BLOCKS):
            nc.vector.tensor_reduce(neg_max[:, b : b + 1], s_ps[b][:], AX.X, ALU.max, negate=True)
            nc.scalar.activation(
                probs[b][:].rearrange("q (u n v) -> q u n v", u=2, v=2),
                s_ps[b][:].rearrange("q (n u v) -> q u n v", u=2, v=2),
                ACT.Exp,
                bias=neg_max[:, b : b + 1],
                scale=1.0,
                accum_out=row_sum[:, b : b + 1],
            )

        vT12 = psum.tile([P, 2, 2, P], F32, name="vT12", tag="turn1")
        vT = [ring.tile([P, 2, P], F32, name="vT0", tag="ring")[:], vT12[:, 0], vT12[:, 1]]
        v_grp = sbuf([P, PACK * I], BF16, "v_grp", "v_pool2")
        for t in (1, 2, 0):
            turn_pairs(vg[t], vT[t], sorted_pairs=(t == 0))
        for t in range(PACK - 1):
            interleave(v_grp[:, t * I : (t + 1) * I], vT[t])

        vg3 = gather_values(3, "t3_0")
        inv_sum = sbuf([P, BLOCKS], F32, "inv_sum", "v_pool3")
        nc.vector.reciprocal(inv_sum[:], row_sum[:])
        v_mx = [quantise(v_grp[:, : 2 * I], "v01", "row_sum")]
        vT3 = ring.tile([P, 2, P], F32, name="vT3", tag="ring")
        turn_pairs(vg3, vT3[:], sorted_pairs=False)
        interleave(v_grp[:, 3 * I :], vT3[:])

        w_grp = []
        for b in range(BLOCKS):
            w_bf = sbuf([P, I], BF16, f"w_bf{b}")
            nc.vector.scalar_tensor_tensor(
                w_bf[:],
                probs[b][:],
                inv_sum[:, b : b + 1],
                size_row[:].rearrange("q u n v -> q (u n v)"),
                ALU.mult,
                ALU.mult,
            )
            wT_ps = psum.tile([P, 2, P], F32, name=f"wT_ps{b}", tag=f"turn{b}")
            w_grp.append(sbuf([P, I], BF16, f"w_grp{b}"))
            turn_pairs(w_bf, wT_ps[:], sorted_pairs=True)
            interleave(w_grp[b][:], wT_ps[:])
        v_mx.append(quantise(v_grp[:, 2 * I :], "v23", "probs0"))
        w_mx = [quantise(w_grp[b][:], f"w{b}") for b in range(BLOCKS)]

        def products(b, bank, tiles):
            for n, t in enumerate(tiles):
                features = slice((t % 2) * P, (t % 2 + 1) * P)
                nc.tensor.matmul_mx(
                    out=bank[:, n, :],
                    lhsT=v_mx[t // 2][0][:, features].bitcast(FP8X4),
                    lhsT_scale=v_mx[t // 2][1][:, features],
                    rhs=w_mx[b][0][:].bitcast(FP8X4),
                    rhs_scale=w_mx[b][1][:],
                    start=True,
                    stop=True,
                )

        out_dealt = out_0.rearrange("(m t) q -> m t q", t=PACK)
        o_sb = [sbuf([P, PACK, P], F32, f"o_sb{b}") for b in range(BLOCKS)]
        o_codes = sbuf([P, Q], U32, "o_codes")
        o_scales = sbuf([P, Q], U8, "o_scales")

        def quantise_result(b, rounded):
            block = slice(b * P, (b + 1) * P)
            nc.vector.quantize_mx(
                out=o_codes[:, block].bitcast(FP8X4),
                scales=o_scales[:, block],
                in_=rounded[:].rearrange("p q t -> p (q t)"),
            )

        o_ps0 = psum.tile([P, PACK, P], F32, name="o_ps0", tag="main0")
        products(0, o_ps0, range(PACK))
        o_bf0 = sbuf([P, P, PACK], BF16, "o_bf0", "w_grp1")
        nc.vector.tensor_copy(o_bf0[:], o_ps0[:].rearrange("p t q -> p q t"))
        o_lo = psum.tile([P, 2, P], F32, name="o_lo", tag="main1")
        o_hi = ring.tile([P, 2, P], F32, name="o_hi", tag="ring")
        products(1, o_lo, (0, 1))
        products(1, o_hi, (2, 3))
        nc.scalar.copy(o_sb[1][:, :2, :], o_lo[:])
        nc.vector.tensor_copy(o_sb[1][:, 2:, :], o_hi[:])
        nc.sync.dma_start(out_dealt[:, :, P:], o_sb[1][:])
        nc.scalar.copy(o_sb[0][:], o_ps0[:])
        nc.sync.dma_start(out_dealt[:, :, :P], o_sb[0][:])
        quantise_result(0, o_bf0)
        o_bf1 = sbuf([P, P, PACK], BF16, "o_bf1")
        for copy, share in (
            (nc.vector.tensor_copy, slice(0, ROUNDED_ON_VECTOR)),
            (nc.scalar.copy, slice(ROUNDED_ON_VECTOR, P)),
        ):
            copy(
                o_bf1[:, share, :].rearrange("p (c j) t -> p c t j", j=RUN),
                o_sb[1][:, :, share].rearrange("p t (c j) -> p c t j", j=RUN),
            )
        quantise_result(1, o_bf1)

        nc.sync.dma_start(out_1[0].rearrange("p c r -> p (c r)").bitcast(I32), o_codes[:].bitcast(I32))
        for g in range(QUADRANTS):
            queue = nc.scalar if g % 2 == 0 else nc.sync
            queue.dma_start(
                out_2[0, 4 * g : 4 * g + 4, :].bitcast(I32), o_scales[32 * g : 32 * g + 4, :].bitcast(I32)
            )
